import numpy as np
import ml_dtypes


def mxq(x, axis, fmt="e4m3"):
    dtype, down = {"e4m3": (ml_dtypes.float8_e4m3fn, 7), "e5m2": (ml_dtypes.float8_e5m2, 14)}[fmt]
    v = np.moveaxis(np.asarray(x, np.float32).astype(ml_dtypes.bfloat16).astype(np.float64), axis, -1)
    blocks = v.reshape(v.shape[:-1] + (-1, 32))
    amax = np.abs(blocks).max(-1, keepdims=True)
    byte = np.maximum(np.where(amax > 0, np.frexp(amax)[1] - 1 + 127, 0) - down, 1)
    scale = np.exp2(byte - 127.0)
    codes = (blocks / scale).astype(np.float32).astype(dtype).astype(np.float64)
    return np.moveaxis((codes * scale).reshape(v.shape), -1, axis)


WIDE = False


def mx_kscale(k):
    if not WIDE:
        return np.ones(k)
    levels = np.array([30, -30])
    if k % 512:
        return np.exp2(np.random.permutation(np.resize(levels, k // 32))).repeat(32)
    a = np.empty((k // 512, 16))
    for p in range(k // 512):
        a[p, :8] = np.random.permutation(np.resize(levels, 8))
        for g in range(8):
            far = levels[np.abs(levels - a[p, g]) >= 10]
            a[p, g + 8] = far[np.random.randint(len(far))]
    return np.exp2(a.ravel()).repeat(32)


def f64(x):
    return np.asarray(x).astype(np.float64)


def striped(idx):
    return np.tile(np.asarray(idx).reshape(-1, 16).T, (8, 1)).astype(np.uint16)


def unstriped(offs):
    return offs[:16].T.reshape(-1).astype(np.int64)


E2M1 = np.array([0.0, 0.5, 1.0, 1.5, 2.0, 3.0, 4.0, 6.0, -0.0, -0.5, -1.0, -1.5, -2.0, -3.0, -4.0, -6.0])


def pack_weight(w, fmt):
    k, n = w.shape
    w = f64(np.asarray(w, np.float32).astype(ml_dtypes.bfloat16)).reshape(k // 32, 32, n)
    amax = np.abs(w).max(1)
    if fmt in ("e4m3", "e5m2"):
        byte = np.frexp(amax)[1] - 1 + 127 - (7 if fmt == "e4m3" else 14)
    else:
        mant, ex = np.frexp(amax / 6.0)
        byte = np.where(mant > 0.5, ex, ex - 1) + 127
    byte = np.clip(np.where(amax > 0, byte, 1), 1, 254)
    scaled = (w * np.exp2(127.0 - byte)[:, None, :]).reshape(k, n).astype(np.float32)
    by_word = np.ascontiguousarray(scaled.reshape(k // 512, 128, 4, n).transpose(0, 1, 3, 2))
    if fmt in ("e4m3", "e5m2"):
        words = by_word.astype(ml_dtypes.float8_e4m3fn if fmt == "e4m3" else ml_dtypes.float8_e5m2).view(np.uint8)
    else:
        c = by_word.astype(ml_dtypes.float4_e2m1fn).view(np.uint8) & 0xF
        words = (c[..., 0::2] | (c[..., 1::2] << 4)).reshape(k // 512, 128, 2 * n)
    return np.ascontiguousarray(words), np.ascontiguousarray(byte.astype(np.uint8).reshape(k // 512, 16, n))


def unpack_weight(words, scales, fmt):
    g, _, n = scales.shape
    words = np.ascontiguousarray(words).reshape(g, 128, n, -1)
    if fmt in ("e4m3", "e5m2"):
        vals = words.view(ml_dtypes.float8_e4m3fn if fmt == "e4m3" else ml_dtypes.float8_e5m2).astype(np.float64)
    else:
        nib = np.empty((g, 128, n, 4), np.uint8)
        nib[..., 0::2] = words & 0xF
        nib[..., 1::2] = words >> 4
        vals = E2M1[nib]
    vals = vals * np.repeat(np.exp2(scales.astype(np.float64) - 127.0), 8, axis=1)[..., None]
    return vals.transpose(0, 1, 3, 2).reshape(g * 512, n)


K, T, Z, J, R, N, C, O = 512, 1024, 1024, 256, 512, 256, 512, 128


def setup_inputs():
    n = np.random.standard_normal
    idx = np.random.permutation(T)[:J]
    idx2 = np.random.permutation(Z)[:J]
    idx3 = np.random.permutation(C)[:J]
    idx4 = np.random.permutation(C)[:J]
    idx5 = np.random.permutation(J)[:O]
    idx6 = np.random.permutation(J)[:O]
    fk = mx_kscale(K)
    fr = mx_kscale(R)
    xtp = pack_weight(n((K, T)) / fk[:, None], "e2m1")
    xop = pack_weight(n((K, Z)) / fk[:, None], "e4m3")
    wp = pack_weight(n((K, R)) * 1 / np.sqrt(K) * fk[:, None] * fr, "e4m3")
    w2p = pack_weight(n((K, R)) * 1 / np.sqrt(K) * fk[:, None] * fr, "e5m2")
    wbp = pack_weight(n((R, N)) * 1 / np.sqrt(R) / fr[:, None], "e2m1")
    wcp = pack_weight(n((R, N)) * 1 / np.sqrt(R) / fr[:, None], "e5m2")
    return {
        "xt_words": xtp[0],
        "xt_scales": xtp[1],
        "xo_words": xop[0],
        "xo_scales": xop[1],
        "w_words": wp[0],
        "w_scales": wp[1],
        "w2_words": w2p[0],
        "w2_scales": w2p[1],
        "wb_words": wbp[0],
        "wb_scales": wbp[1],
        "wc_words": wcp[0],
        "wc_scales": wcp[1],
        "so": (np.random.uniform(0.5, 1.6, (N, 1))).astype(np.float32),
        "sp": (np.random.uniform(0.5, 1.6, (N, 1))).astype(np.float32),
        "offs": striped(idx),
        "offs2": striped(idx2),
        "offs3": striped(idx3),
        "offs4": striped(idx4),
        "offs5": striped(idx5),
        "offs6": striped(idx6),
    }


def reference(xt_words, xt_scales, xo_words, xo_scales, w_words, w_scales, w2_words, w2_scales, wb_words, wb_scales, wc_words, wc_scales, so, sp, offs, offs2, offs3, offs4, offs5, offs6):
    idx = unstriped(offs)
    idx2 = unstriped(offs2)
    idx3 = unstriped(offs3)
    idx4 = unstriped(offs4)
    idx5 = unstriped(offs5)
    idx6 = unstriped(offs6)
    xtu = unpack_weight(xt_words, xt_scales, "e2m1")
    xou = unpack_weight(xo_words, xo_scales, "e4m3")
    wu = unpack_weight(w_words, w_scales, "e4m3")
    w2u = unpack_weight(w2_words, w2_scales, "e5m2")
    wbu = unpack_weight(wb_words, wb_scales, "e2m1")
    wcu = unpack_weight(wc_words, wc_scales, "e5m2")
    xtidxg = xtu[:, idx]
    xoidx2g = xou[:, idx2]
    a = wu.T @ xtidxg + w2u.T @ xoidx2g
    b = w2u.T @ xtidxg + wu.T @ xoidx2g
    hid = np.maximum(a, b)
    hidq = mxq(hid, 0, "e5m2")
    p = wbu.T @ hidq
    q = wcu.T @ hidq
    pw = np.zeros((N, C))
    pw[:, idx3] = p
    m0 = np.maximum(pw[:, idx4] * f64(so), q)
    y = m0[:, idx5] - m0[:, idx6] * f64(sp)
    return y

from contextlib import ExitStack

import concourse.mybir as mybir
from concourse.masks import make_identity

FLOPS = 671088640

F32 = mybir.dt.float32
BF16 = mybir.dt.bfloat16
I32 = mybir.dt.int32
U32 = mybir.dt.uint32
U16 = mybir.dt.uint16
U8 = mybir.dt.uint8
E4M3 = mybir.dt.float8_e4m3fn_x4
E5M2 = mybir.dt.float8_e5m2_x4
E2M1 = mybir.dt.float4_e2m1fn_x4
MAX = mybir.AluOpType.max
SUBTRACT = mybir.AluOpType.subtract
COPY = mybir.ActivationFunctionType.Copy

P = 128
T, J, R, N, C, O = 1024, 256, 512, 256, 512, 128


def tile_list_outcomechain_crossed_kernel(
    tc, xt_words, xt_scales, xo_words, xo_scales, w_words, w_scales, w2_words, w2_scales,
    wb_words, wb_scales, wc_words, wc_scales, so, sp, offs, offs2, offs3, offs4, offs5, offs6, out,
):
    nc = tc.nc
    with ExitStack() as ctx:
        sb = ctx.enter_context(tc.tile_pool(name="sb", bufs=1))
        ps = ctx.enter_context(tc.psum_pool(name="ps", bufs=1))

        def tile(name, shape, dtype, tag=None):
            return sb.tile(shape, dtype, name=name, tag=tag or name, align_bytes=64)

        def words(dram):
            return dram[0].rearrange("p n t -> p (n t)").bitcast(I32)

        def load_list(name, dram):
            t = sb.tile(list(dram.shape), U16, name=name)
            nc.sync.dma_start(t[:], dram)
            return t

        def load_scale_rows(queue, stage, dram, a, first=0):
            width = dram.shape[2] // 4
            rows = dram[0].bitcast(I32).rearrange("(h a r) n -> a r h n", h=2, a=2, r=4)[a]
            halves = stage[32 * a : 32 * a + 4, :].bitcast(I32).rearrange("p (h n) -> p h n", h=2)
            queue.dma_start(halves[:, :, first : first + width], rows)

        def lift(plane, stage):
            half = stage.shape[1] // 2
            nc.vector.tensor_copy(plane[64:128, 0:half].bitcast(I32), stage[0:64, half : 2 * half].bitcast(I32))

        xt_stage = tile("xt_stage", [64, 2 * T], U8)
        w_planes = tile("w_planes", [P, 2 * R], U8)
        xo_stage = tile("xo_stage", [64, 2 * T], U8)
        w2_planes = tile("w2_planes", [P, 2 * R], U8)
        out_planes = tile("out_planes", [P, 4 * N], U8)
        for t in (xt_stage, w_planes, w2_planes, xo_stage, out_planes):
            nc.vector.memset(t[0:64, :].bitcast(I32), 0)
        w_plane, w2_plane = w_planes[:, 0:R], w2_planes[:, 0:R]
        wb_plane, wc_plane = out_planes[:, 0:N], out_planes[:, N : 2 * N]
        xt_bytes = tile("xt_bytes", [P, T], U8)
        xo_bytes = tile("xo_bytes", [P, T], U8)

        xt_table = tile("xt_table", [P, T], U16)
        xo_table = tile("xo_table", [P, T], I32)
        w_sb = tile("w_sb", [P, R], I32)
        w2_sb = tile("w2_sb", [P, R], I32)
        wb_sb = tile("wb_sb", [P, 2 * N], U8)
        wc_sb = tile("wc_sb", [P, N], I32)

        identity = tile("identity", [P, P], F32)
        make_identity(nc, identity[:])
        list1 = load_list("list1", offs)
        nc.sync.dma_start(xt_table[:].bitcast(I32), xt_words[0].bitcast(I32))
        for a in range(2):
            load_scale_rows(nc.sync, xt_stage, xt_scales, a)
        for a in range(2):
            load_scale_rows(nc.sync, w_planes, w_scales, a)
        nc.sync.dma_start(w_sb[:], words(w_words))
        nc.sync.dma_start(w2_sb[:], words(w2_words))
        list2 = load_list("list2", offs2)
        for a in range(2):
            load_scale_rows(nc.sync, w2_planes, w2_scales, a)
        for a in range(2):
            load_scale_rows(nc.sync, xo_stage, xo_scales, a)
        nc.sync.dma_start(xo_table[:], words(xo_words))
        for a in range(2):
            load_scale_rows(nc.sync, out_planes, wb_scales, a)
        for a in range(2):
            load_scale_rows(nc.sync, out_planes, wc_scales, a, N // 4)
        nc.sync.dma_start(wb_sb[:].bitcast(I32), wb_words[0].bitcast(I32))
        list3 = load_list("list3", offs3)
        nc.sync.dma_start(wc_sb[:], words(wc_words))
        list4 = load_list("list4", offs4)
        so_sb = tile("so_sb", [P, 2], F32)
        sp_sb = tile("sp_sb", [P, 2], F32)
        with nc.allow_non_contiguous_dma(reason="one value a partition"):
            nc.sync.dma_start(so_sb[:], so.rearrange("(g p) o -> p (g o)", p=P))
            nc.sync.dma_start(sp_sb[:], sp.rearrange("(g p) o -> p (g o)", p=P))
        list6 = load_list("list6", offs6)
        list5 = load_list("list5", offs5)

        def spread(window, stage):
            nc.vector.tensor_copy(window[0:64, :].bitcast(I32), stage[:, 0:T].bitcast(I32))
            lift(window, stage)

        spread(xt_bytes, xt_stage)
        lift(w_planes, w_planes)

        def gather_half(name, dtype, window, lst, h):
            t = tile("%s%d" % (name, h), [P, P], dtype)
            nc.vector.tensor_copy(t[:], window.indirect(lst[:, 8 * h : 8 * h + 8]))
            return t

        xt_s, xt_w, xo_s, xo_w = [], [], [], []
        for h in range(2):
            xt_w.append(gather_half("xt_w", U16, xt_table[:], list1, h))
            xt_s.append(gather_half("xt_s", U8, xt_bytes[:], list1, h))
        lift(w2_planes, w2_planes)
        spread(xo_bytes, xo_stage)
        for h in range(2):
            xo_s.append(gather_half("xo_s", U8, xo_bytes[:], list2, h))
            xo_w.append(gather_half("xo_w", U32, xo_table[:].bitcast(U32), list2, h))

        lift(out_planes, out_planes)
        boards = [tile("board%d" % g, [P, C], F32, tag=("xo_table", "xo_bytes")[g]) for g in range(2)]
        for g in range(2):
            nc.gpsimd.memset(boards[g][:], 0.0)

        a_ps = [ps.tile([P, R], F32, name="a%d" % h, tag="a%d" % h) for h in range(2)]
        b_ps = [ps.tile([P, R], F32, name="b%d" % h, tag="b%d" % h) for h in range(2)]
        w_op = (w_sb[:].bitcast(E4M3), w_plane)
        w2_op = (w2_sb[:].bitcast(E5M2), w2_plane)

        def first_stage(acc, codes, scales, weight, start):
            nc.tensor.matmul_mx(out=acc[:], lhsT=codes, lhsT_scale=scales[:], rhs=weight[0], rhs_scale=weight[1],
                                start=start, stop=not start)

        for acc, weight in ((a_ps, w_op), (b_ps, w2_op)):
            for h in range(2):
                first_stage(acc[h], xt_w[h][:].bitcast(E2M1), xt_s[h], weight, True)
        for h in range(2):
            for acc, weight in ((b_ps, w_op), (a_ps, w2_op)):
                first_stage(acc[h], xo_w[h][:].bitcast(E4M3), xo_s[h], weight, False)

        hid_codes = tile("hid_codes", [P, J], U32)
        hid_plane = tile("hid_plane", [P, J], U8)
        p_sb = tile("p_sb", [P, 2, 2, P], F32)
        for h in range(2):
            turned = ps.tile([P, 2, P], F32, name="turned%d" % h, tag="turned%d" % h)
            for u in range(2):
                b_sb = tile("b_sb%d%d" % (h, u), [P, P, 2], F32)
                nc.scalar.copy(b_sb[:], b_ps[h][:].rearrange("j (p u e) -> j u p e", u=2, e=2)[:, u])
                hid_t = tile("hid_t%d%d" % (h, u), [P, P, 2], BF16)
                nc.vector.tensor_tensor(hid_t[:], a_ps[h][:].rearrange("j (p u e) -> j u p e", u=2, e=2)[:, u], b_sb[:], MAX)
                nc.tensor.transpose(turned[:, u, :], hid_t[:].rearrange("j p e -> j (p e)").bitcast(F32), identity[:])
            hid = tile("hid%d" % h, [P, 4 * P], BF16)
            nc.scalar.copy(hid[:].bitcast(F32).rearrange("p (j u) -> p j u", u=2), turned[:].rearrange("p u j -> p j u"))
            cols = slice(h * P, (h + 1) * P)
            nc.vector.quantize_mx(out=hid_codes[:, cols].bitcast(E5M2), scales=hid_plane[:, cols], in_=hid[:])
            for g in range(2):
                p_ps = ps.tile([P, P], F32, name="p%d%d" % (h, g), tag=("a%d" if g == 0 else "b%d") % h)
                nc.tensor.matmul_mx(out=p_ps[:], lhsT=wb_sb[:, 2 * g * P : 2 * (g + 1) * P].bitcast(E2M1),
                                    lhsT_scale=wb_plane[:, g * P : (g + 1) * P],
                                    rhs=hid_codes[:, cols].bitcast(E5M2), rhs_scale=hid_plane[:, cols], start=True, stop=True)
                scattered = boards[g][:].indirect(list3[:, 8 * h : 8 * h + 8])
                if g == 0:
                    nc.vector.tensor_copy(p_sb[:, h, g, :], p_ps[:])
                    nc.vector.tensor_copy(scattered, p_sb[:, h, g, :])
                else:
                    nc.scalar.copy(p_sb[:, h, g, :], p_ps[:])
                    nc.scalar.activation(scattered, p_sb[:, h, g, :], COPY)

        for g in (1, 0):
            q_ps = ps.tile([P, J], F32, name="q%d" % g, tag="q%d" % g)
            nc.tensor.matmul_mx(out=q_ps[:], lhsT=wc_sb[:, g * P : (g + 1) * P].bitcast(E5M2),
                                lhsT_scale=wc_plane[:, g * P : (g + 1) * P],
                                rhs=hid_codes[:].bitcast(E5M2), rhs_scale=hid_plane[:], start=True, stop=True)
            looked = tile("looked%d" % g, [P, J], F32)
            nc.scalar.activation(looked[:], boards[g][:].indirect(list4[:]), COPY, scale=so_sb[:, g : g + 1])
            m0 = tile("m0_%d" % g, [P, J], F32)
            nc.vector.tensor_tensor(m0[:], looked[:], q_ps[:], MAX)
            taken = tile("taken%d" % g, [P, O], F32)
            nc.scalar.activation(taken[:], m0[:].indirect(list6[:]), COPY, scale=sp_sb[:, g : g + 1])
            kept = tile("kept%d" % g, [P, O], F32)
            nc.vector.tensor_copy(kept[:], m0[:].indirect(list5[:]))
            result = tile("result%d" % g, [P, O], F32)
            nc.vector.tensor_tensor(result[:], kept[:], taken[:], SUBTRACT)
            nc.sync.dma_start(out[g * P : (g + 1) * P, :], result[:])
